import numpy as np
import ml_dtypes


def mxq(x, axis, fmt="e4m3"):
    dtype, down = {"e4m3": (ml_dtypes.float8_e4m3fn, 7), "e5m2": (ml_dtypes.float8_e5m2, 14)}[fmt]
    v = np.moveaxis(np.asarray(x, np.float32).astype(ml_dtypes.bfloat16).astype(np.float64), axis, -1)
    blocks = v.reshape(v.shape[:-1] + (-1, 32))
    amax = np.abs(blocks).max(-1, keepdims=True)
    byte = np.maximum(np.where(amax > 0, np.frexp(amax)[1] - 1 + 127, 0) - down, 1)
    scale = np.exp2(byte - 127.0)
    codes = (blocks / scale).astype(np.float32).astype(dtype).astype(np.float64)
    return np.moveaxis((codes * scale).reshape(v.shape), -1, axis)


WIDE = False


def mx_kscale(k):
    if not WIDE:
        return np.ones(k)
    levels = np.array([30, -30])
    if k % 512:
        return np.exp2(np.random.permutation(np.resize(levels, k // 32))).repeat(32)
    a = np.empty((k // 512, 16))
    for p in range(k // 512):
        a[p, :8] = np.random.permutation(np.resize(levels, 8))
        for g in range(8):
            far = levels[np.abs(levels - a[p, g]) >= 10]
            a[p, g + 8] = far[np.random.randint(len(far))]
    return np.exp2(a.ravel()).repeat(32)


def f64(x):
    return np.asarray(x).astype(np.float64)


E2M1 = np.array([0.0, 0.5, 1.0, 1.5, 2.0, 3.0, 4.0, 6.0, -0.0, -0.5, -1.0, -1.5, -2.0, -3.0, -4.0, -6.0])


def pack_weight(w, fmt):
    k, n = w.shape
    w = f64(np.asarray(w, np.float32).astype(ml_dtypes.bfloat16)).reshape(k // 32, 32, n)
    amax = np.abs(w).max(1)
    if fmt == "e4m3":
        byte = np.frexp(amax)[1] - 1 + 127 - 7
    else:
        mant, ex = np.frexp(amax / 6.0)
        byte = np.where(mant > 0.5, ex, ex - 1) + 127
    byte = np.clip(np.where(amax > 0, byte, 1), 1, 254)
    scaled = (w * np.exp2(127.0 - byte)[:, None, :]).reshape(k, n).astype(np.float32)
    by_word = np.ascontiguousarray(scaled.reshape(k // 512, 128, 4, n).transpose(0, 1, 3, 2))
    if fmt == "e4m3":
        words = by_word.astype(ml_dtypes.float8_e4m3fn).view(np.uint8)
    else:
        c = by_word.astype(ml_dtypes.float4_e2m1fn).view(np.uint8) & 0xF
        words = (c[..., 0::2] | (c[..., 1::2] << 4)).reshape(k // 512, 128, 2 * n)
    return np.ascontiguousarray(words), np.ascontiguousarray(byte.astype(np.uint8).reshape(k // 512, 16, n))


def unpack_weight(words, scales, fmt):
    g, _, n = scales.shape
    words = np.ascontiguousarray(words).reshape(g, 128, n, -1)
    if fmt == "e4m3":
        vals = words.view(ml_dtypes.float8_e4m3fn).astype(np.float64)
    else:
        nib = np.empty((g, 128, n, 4), np.uint8)
        nib[..., 0::2] = words & 0xF
        nib[..., 1::2] = words >> 4
        vals = E2M1[nib]
    vals = vals * np.repeat(np.exp2(scales.astype(np.float64) - 127.0), 8, axis=1)[..., None]
    return vals.transpose(0, 1, 3, 2).reshape(g * 512, n)


def bf(x):
    return np.asarray(x, np.float32).astype(ml_dtypes.bfloat16)


def planes(Y):
    r, m = Y.shape
    b = f64(bf(Y)).reshape(r // 32, 32, m)
    amax = np.abs(b).max(1)
    byte = np.clip(np.where(amax > 0, np.frexp(amax)[1] - 1 + 127 - 7, 1), 1, 254)
    codes = (b * np.exp2(127.0 - byte)[:, None, :]).reshape(r, m).astype(np.float32).astype(ml_dtypes.float8_e4m3fn).view(np.uint8)
    words = codes.reshape(r // 512, 128, 4, m).transpose(0, 1, 3, 2)
    return np.ascontiguousarray(words), np.ascontiguousarray(byte.astype(np.uint8).reshape(r // 512, 16, m))


K, T, N = 1024, 512, 512


def setup_inputs():
    n = np.random.standard_normal
    fk = mx_kscale(K)
    wap = pack_weight(n((K, N)) * 1 / np.sqrt(K) * fk[:, None], "e4m3")
    wbp = pack_weight(n((K, N)) * 1 / np.sqrt(K) * fk[:, None], "e2m1")
    wcp = pack_weight(n((K, N)) * 1 / np.sqrt(K) * fk[:, None], "e4m3")
    return {
        "xf": (n((K, T))).astype(np.float32),
        "fa": (np.random.uniform(0.5, 2.0, (K, 1)) / fk[:, None]).astype(np.float32),
        "fb": (np.random.uniform(0.5, 2.0, (K, 1)) / fk[:, None]).astype(np.float32),
        "fd": (np.random.uniform(0.5, 2.0, (K, 1)) / fk[:, None]).astype(np.float32),
        "wa_words": wap[0],
        "wa_scales": wap[1],
        "wb_words": wbp[0],
        "wb_scales": wbp[1],
        "wc_words": wcp[0],
        "wc_scales": wcp[1],
    }


def reference(xf, fa, fb, fd, wa_words, wa_scales, wb_words, wb_scales, wc_words, wc_scales):
    wau = unpack_weight(wa_words, wa_scales, "e4m3")
    wbu = unpack_weight(wb_words, wb_scales, "e2m1")
    wcu = unpack_weight(wc_words, wc_scales, "e4m3")
    ua = f64(xf) * f64(fa)
    x1 = np.pad(f64(xf), ((0, 0), (1, 0)))[:, :T]
    ub = x1 * f64(fb)
    x2 = np.pad(f64(xf), ((0, 0), (2, 0)))[:, :T]
    uc = x2 * f64(fd)
    uaq = mxq(ua, 0, "e4m3")
    ubq = mxq(ub, 0, "e5m2")
    ucq = mxq(uc, 0, "e4m3")
    z = wau.T @ uaq + wbu.T @ ubq + wcu.T @ ucq
    y = np.maximum(z, 0.0)
    words, scales = planes(y)
    return y, words, scales

@@ -1,0 +1,209 @@
+from contextlib import ExitStack
+
+import concourse.mybir as mybir
+
+K, T, N = 1024, 512, 512
+FLOPS = 3 * 2 * K * T * N
+
+F32 = mybir.dt.float32
+BF16 = mybir.dt.bfloat16
+I32 = mybir.dt.int32
+U8 = mybir.dt.uint8
+E4M3 = mybir.dt.float8_e4m3fn_x4
+E5M2 = mybir.dt.float8_e5m2_x4
+E2M1 = mybir.dt.float4_e2m1fn_x4
+ACT = mybir.ActivationFunctionType
+ALU = mybir.AluOpType
+
+P = 128
+PACK = 4
+PASSES = K // (P * PACK)
+HALF = T // 2
+RUN = 4
+SHIFT = {"a": 0, "b": 1, "c": 2}
+SCALE_ROW = {"a": 4, "b": 0, "c": 8}
+U_FORMAT = {"a": E4M3, "b": E5M2, "c": E4M3}
+
+
+def tile_mix_three_windows_one_sum_pl_kernel(
+    tc, xf, fa, fb, fd, wa_words, wa_scales, wb_words, wb_scales, wc_words, wc_scales, out_0, out_1, out_2
+):
+    nc = tc.nc
+    with ExitStack() as ctx:
+        sb = ctx.enter_context(tc.tile_pool(name="sb", bufs=1))
+        ps = ctx.enter_context(tc.psum_pool(name="ps", bufs=1))
+        ctx.enter_context(tc.manual_schedule())
+
+        def tile(name, shape, dtype):
+            return sb.tile(shape, dtype, name=name, align_bytes=64)
+
+        ops = [(w, g) for w in "abc" for g in range(PASSES)]
+        factor = {w: tile("f_" + w, [P, PASSES, PACK], F32) for w in "abc"}
+        x_first = [tile("x0_%d" % j, [P, T], F32) for j in range(PACK)]
+        x_second = [tile("x1_%d" % h, [P, 2, T], F32) for h in range(2)]
+        rows = {o: tile("rows_%s%d" % o, [P, PACK, T], BF16) for o in ops}
+        woven = {o: tile("woven_%s%d" % o, [P, T, PACK], BF16) for o in ops}
+        u_codes = {o: tile("codes_%s%d" % o, [P, T], I32) for o in ops}
+        u_scales = {o: tile("scales_%s%d" % o, [P, T], U8) for o in ops}
+        w_raw = {
+            "a": tile("wa_raw", [P, PASSES, N], I32),
+            "b": tile("wb_raw", [P, PASSES, 2 * N], U8),
+            "c": tile("wc_raw", [P, PASSES, N], I32),
+        }
+        w_dealt = {}
+        for w, g in ops:
+            if w == "b":
+                w_dealt[w, g] = tile("dealt_%s%d" % (w, g), [P, PACK, 2 * P], U8)
+            else:
+                w_dealt[w, g] = tile("dealt_%s%d" % (w, g), [P, PACK, P], I32)
+        ws_raw = tile("ws_raw", [P, PASSES, N], U8)
+        ws_dealt = tile("ws_dealt", [P, PASSES, PACK, P], U8)
+        zeros = tile("zeros", [P, PACK, 2], F32)
+        y = tile("y", [P, PACK, T], F32)
+        y_woven = tile("y_woven", [P, T, PACK], BF16)
+        y_codes = tile("y_codes", [P, T], I32)
+        y_scales = tile("y_scales", [P, T], U8)
+        acc = [ps.tile([P, T], F32, name="acc%d" % r) for r in range(PACK)]
+
+        def x_row(g, j):
+            return x_first[j][:] if g == 0 else x_second[j // 2][:, j % 2, :]
+
+        def load_scales(eng, w, src, quadrants):
+            k = SCALE_ROW[w]
+            for r in quadrants:
+                eng.dma_start(
+                    out=ws_raw[k + r : P : 32].bitcast(I32),
+                    in_=src.rearrange("g (q r) n -> r q g n", r=4)[r].bitcast(I32),
+                )
+
+        def multiply(on_vector, w, g, j):
+            s = SHIFT[w]
+            dst = rows[w, g][:, j, s:T]
+            src = x_row(g, j)[:, 0 : T - s]
+            f = factor[w][:, g, j : j + 1]
+            if on_vector:
+                nc.vector.tensor_scalar(out=dst, in0=src, scalar1=f, scalar2=None, op0=ALU.mult)
+            else:
+                nc.scalar.activation(out=dst, in_=src, func=ACT.Copy, scale=f)
+
+        def weave(on_vector, dst, src, t0, t1):
+            o = dst[:, t0:t1, :].rearrange("p (c i) j -> p c j i", i=RUN)
+            i = src[:, :, t0:t1].rearrange("p j (c i) -> p c j i", i=RUN)
+            if on_vector:
+                nc.vector.tensor_copy(out=o, in_=i)
+            else:
+                nc.scalar.copy(out=o, in_=i)
+
+        def quantise(codes, scales, src, fmt, t0, t1):
+            nc.vector.quantize_mx(
+                out=codes[:, t0:t1].bitcast(fmt),
+                scales=scales[:, t0:t1],
+                in_=src[:, t0:t1, :].rearrange("p t j -> p (t j)"),
+            )
+
+        def quantise_u(w, g, t0=0, t1=T):
+            quantise(u_codes[w, g], u_scales[w, g], woven[w, g], U_FORMAT[w], t0, t1)
+
+        def deal_words(w, g):
+            if w == "b":
+                nc.vector.tensor_copy(
+                    out=w_dealt[w, g][:].rearrange("p r (m e) -> p r m e", e=2),
+                    in_=w_raw[w][:, g, :].rearrange("p (m r e) -> p r m e", r=PACK, e=2),
+                )
+            else:
+                nc.vector.tensor_copy(
+                    out=w_dealt[w, g][:].rearrange("p r (c i) -> p c r i", i=RUN),
+                    in_=w_raw[w][:, g, :].rearrange("p (c i r) -> p c r i", r=PACK, i=RUN),
+                )
+
+        def matmuls(w, g, first, last, t0=0, t1=T):
+            for r in range(PACK):
+                nc.tensor.matmul_mx(
+                    out=acc[r][:, t0:t1],
+                    lhsT=w_dealt[w, g][:, r, :].bitcast(E2M1 if w == "b" else E4M3),
+                    lhsT_scale=ws_dealt[SCALE_ROW[w] : P, g, r, :],
+                    rhs=u_codes[w, g][:, t0:t1].bitcast(U_FORMAT[w]),
+                    rhs_scale=u_scales[w, g][:, t0:t1],
+                    start=first,
+                    stop=last,
+                )
+
+        x_by_row = xf.rearrange("(g p j) t -> g p j t", g=PASSES, j=PACK)
+        for j in range(PACK):
+            nc.sync.dma_start(out=x_first[j][:], in_=x_by_row[0, :, j, :])
+            if j == 0:
+                for w, src in (("a", fa), ("b", fb), ("c", fd)):
+                    nc.scalar.dma_start(
+                        out=factor[w][:], in_=src.rearrange("(g p j) o -> p g (j o)", g=PASSES, j=PACK)
+                    )
+        nc.gpsimd.memset(ws_raw[:].bitcast(I32), 0)
+        load_scales(nc.gpsimd, "a", wa_scales, range(4))
+        nc.sync.dma_start(out=x_second[0][:], in_=x_by_row[1, :, 0:2, :])
+        load_scales(nc.sync, "b", wb_scales, range(4))
+        nc.sync.dma_start(out=w_raw["b"][:].bitcast(I32), in_=wb_words.rearrange("g p c -> p g c").bitcast(I32))
+        load_scales(nc.sync, "c", wc_scales, range(3))
+        nc.sync.dma_start(out=x_second[1][:], in_=x_by_row[1, :, 2:4, :])
+        load_scales(nc.sync, "c", wc_scales, range(3, 4))
+        nc.sync.dma_start(out=w_raw["c"][:], in_=wc_words.rearrange("g p n e -> p g (n e)").bitcast(I32))
+        nc.sync.dma_start(out=w_raw["a"][:], in_=wa_words.rearrange("g p n e -> p g (n e)").bitcast(I32))
+
+        nc.vector.memset(zeros[:], 0.0)
+        for w in "bc":
+            nc.vector.memset(rows[w, 0][:, :, 0:2], 0.0)
+            nc.scalar.activation(out=rows[w, 1][:, :, 0:2], in_=zeros[:], func=ACT.Copy)
+
+        for j in range(PACK):
+            multiply(False, "a", 0, j)
+            multiply(True, "b", 0, j)
+            multiply(True, "c", 0, j)
+        weave(False, woven["a", 0], rows["a", 0], 0, T)
+        weave(True, woven["b", 0], rows["b", 0], 0, T)
+        weave(True, woven["c", 0], rows["c", 0], 0, T)
+        deal_words("b", 0)
+        quantise_u("b", 0)
+        nc.vector.tensor_copy(out=ws_dealt[:], in_=ws_raw[:].rearrange("p g (m r) -> p g r m", r=PACK))
+        matmuls("b", 0, True, False)
+        quantise_u("c", 0)
+        for w, js in (("b", (0, 1)), ("c", (0, 1)), ("b", (2, 3)), ("c", (2, 3)), ("a", range(PACK))):
+            for j in js:
+                multiply(False, w, 1, j)
+        deal_words("c", 0)
+        matmuls("c", 0, False, False)
+        quantise_u("a", 0)
+        deal_words("a", 0)
+        matmuls("a", 0, False, False)
+        weave(True, woven["b", 1], rows["b", 1], 0, T)
+        deal_words("b", 1)
+        quantise_u("b", 1)
+        matmuls("b", 1, False, False)
+        weave(True, woven["c", 1], rows["c", 1], 0, T)
+        deal_words("c", 1)
+        quantise_u("c", 1)
+        matmuls("c", 1, False, False)
+        deal_words("a", 1)
+        weave(False, woven["a", 1], rows["a", 1], 0, HALF)
+        quantise_u("a", 1, 0, HALF)
+        matmuls("a", 1, False, False, 0, HALF)
+        weave(False, woven["a", 1], rows["a", 1], HALF, T)
+        quantise_u("a", 1, HALF, T)
+        matmuls("a", 1, False, True, HALF, T)
+
+        out_rows = out_0.rearrange("(p r) t -> p r t", r=PACK)
+        for r in range(PACK):
+            if r % 2 == 0:
+                nc.scalar.activation(out=y[:, r, :], in_=acc[r][:], func=ACT.Relu)
+            else:
+                nc.vector.tensor_scalar(out=y[:, r, :], in0=acc[r][:], scalar1=0.0, scalar2=None, op0=ALU.max)
+                nc.sync.dma_start(out=out_rows[:, r - 1 : r + 1, :], in_=y[:, r - 1 : r + 1, :])
+        weave(True, y_woven, y, 0, HALF)
+        weave(False, y_woven, y, HALF, HALF + P)
+        weave(True, y_woven, y, HALF + P, T)
+        words_out = out_1[0].rearrange("p t e -> p (t e)").bitcast(I32)
+        for t0 in (0, HALF):
+            quantise(y_codes, y_scales, y_woven, E4M3, t0, t0 + HALF)
+            nc.sync.dma_start(out=words_out[:, t0 : t0 + HALF], in_=y_codes[:, t0 : t0 + HALF])
+        for q in range(4):
+            eng = nc.scalar if q < 2 else nc.sync
+            eng.dma_start(
+                out=out_2[0, 4 * q : 4 * q + 4, :].bitcast(I32), in_=y_scales[32 * q : 32 * q + 4, :].bitcast(I32)
+            )

@@ -1,6 +1,7 @@
 from contextlib import ExitStack
 
 import concourse.mybir as mybir
+from concourse.masks import make_identity
 
 K, T, N = 1024, 512, 512
 FLOPS = 3 * 2 * K * T * N
@@ -19,10 +20,11 @@ P = 128
 PACK = 4
 PASSES = K // (P * PACK)
 HALF = T // 2
-RUN = 4
+HALO = 2
+LEAD = 8
 SHIFT = {"a": 0, "b": 1, "c": 2}
-SCALE_ROW = {"a": 4, "b": 0, "c": 8}
 U_FORMAT = {"a": E4M3, "b": E5M2, "c": E4M3}
+W_FORMAT = {"a": E4M3, "b": E2M1, "c": E4M3}
 
 
 def tile_mix_three_windows_one_sum_pl_kernel(
@@ -31,68 +33,90 @@ def tile_mix_three_windows_one_sum_pl_kernel(
     nc = tc.nc
     with ExitStack() as ctx:
         sb = ctx.enter_context(tc.tile_pool(name="sb", bufs=1))
-        ps = ctx.enter_context(tc.psum_pool(name="ps", bufs=1))
+        acc_pool = ctx.enter_context(tc.psum_pool(name="acc", bufs=1))
+        turn_pool = ctx.enter_context(tc.psum_pool(name="turn", bufs=1))
         ctx.enter_context(tc.manual_schedule())
 
         def tile(name, shape, dtype):
             return sb.tile(shape, dtype, name=name, align_bytes=64)
 
         ops = [(w, g) for w in "abc" for g in range(PASSES)]
-        factor = {w: tile("f_" + w, [P, PASSES, PACK], F32) for w in "abc"}
-        x_first = [tile("x0_%d" % j, [P, T], F32) for j in range(PACK)]
-        x_second = [tile("x1_%d" % h, [P, 2, T], F32) for h in range(2)]
-        rows = {o: tile("rows_%s%d" % o, [P, PACK, T], BF16) for o in ops}
+        factor = {w: tile("f_" + w, [P, PASSES, 2 * PACK], F32) for w in "abc"}
+        x_head = [tile("x_head%d" % pair, [P, 2, HALF], F32) for pair in range(2)]
+        x_early = tile("x_early", [P, PACK, HALF], F32)
+        x_late = [tile("x_late%d" % g, [P, PACK, LEAD + HALF], F32) for g in range(PASSES)]
+        rows = {o: tile("rows_%s%d" % o, [P, PACK, T], BF16) for o in ops if o != ("c", 1)}
         woven = {o: tile("woven_%s%d" % o, [P, T, PACK], BF16) for o in ops}
         u_codes = {o: tile("codes_%s%d" % o, [P, T], I32) for o in ops}
         u_scales = {o: tile("scales_%s%d" % o, [P, T], U8) for o in ops}
-        w_raw = {
-            "a": tile("wa_raw", [P, PASSES, N], I32),
-            "b": tile("wb_raw", [P, PASSES, 2 * N], U8),
-            "c": tile("wc_raw", [P, PASSES, N], I32),
-        }
-        w_dealt = {}
-        for w, g in ops:
-            if w == "b":
-                w_dealt[w, g] = tile("dealt_%s%d" % (w, g), [P, PACK, 2 * P], U8)
-            else:
-                w_dealt[w, g] = tile("dealt_%s%d" % (w, g), [P, PACK, P], I32)
-        ws_raw = tile("ws_raw", [P, PASSES, N], U8)
-        ws_dealt = tile("ws_dealt", [P, PASSES, PACK, P], U8)
-        zeros = tile("zeros", [P, PACK, 2], F32)
-        y = tile("y", [P, PACK, T], F32)
+        w_words = {w: tile("words_" + w, [P, PASSES, (2 if w == "b" else 4) * N], U8) for w in "abc"}
+        w_scales = {w: tile("wscales_" + w, [P, PASSES, N], U8) for w in "abc"}
+        zeros = tile("zeros", [P, PACK, HALO], F32)
+        identity = tile("identity", [P, P], F32)
+        z_relu = [tile("z_relu%d" % c, [P, PACK, P], F32) for c in range(4)]
+        y = [tile("y%d" % c, [P, PACK, P], F32) for c in range(4)]
         y_woven = tile("y_woven", [P, T, PACK], BF16)
         y_codes = tile("y_codes", [P, T], I32)
         y_scales = tile("y_scales", [P, T], U8)
-        acc = [ps.tile([P, T], F32, name="acc%d" % r) for r in range(PACK)]
+        acc = [acc_pool.tile([P, N], F32, name="acc%d" % c) for c in range(4)]
+        turned = [turn_pool.tile([P, PACK, P], F32, name="turned%d" % c) for c in range(4)]
 
-        def x_row(g, j):
-            return x_first[j][:] if g == 0 else x_second[j // 2][:, j % 2, :]
+        def x_rows(g, t0, t1):
+            if t1 > HALF:
+                return x_late[g][:, :, LEAD + t0 - HALF : LEAD + t1 - HALF]
+            return x_early[:, :, t0:t1]
 
-        def load_scales(eng, w, src, quadrants):
-            k = SCALE_ROW[w]
-            for r in quadrants:
-                eng.dma_start(
-                    out=ws_raw[k + r : P : 32].bitcast(I32),
+        def x_row(g, j, t0, t1):
+            if g == 0 and t1 <= HALF:
+                return x_head[j // 2][:, j % 2, t0:t1]
+            return x_rows(g, t0, t1)[:, j, :]
+
+        def load_scales(w, src, rows_of_quadrant):
+            for r in rows_of_quadrant:
+                nc.sync.dma_start(
+                    out=w_scales[w][r:P:32].bitcast(I32),
                     in_=src.rearrange("g (q r) n -> r q g n", r=4)[r].bitcast(I32),
                 )
 
-        def multiply(on_vector, w, g, j):
+        def load_words(w, src):
+            nc.sync.dma_start(out=w_words[w][:].bitcast(I32), in_=src.bitcast(I32))
+
+        def multiply(on_vector, w, g, j, t0, t1):
             s = SHIFT[w]
-            dst = rows[w, g][:, j, s:T]
-            src = x_row(g, j)[:, 0 : T - s]
+            t0 = max(t0, s)
+            dst = rows[w, g][:, j, t0:t1]
+            src = x_row(g, j, t0 - s, t1 - s)
             f = factor[w][:, g, j : j + 1]
             if on_vector:
                 nc.vector.tensor_scalar(out=dst, in0=src, scalar1=f, scalar2=None, op0=ALU.mult)
             else:
                 nc.scalar.activation(out=dst, in_=src, func=ACT.Copy, scale=f)
 
-        def weave(on_vector, dst, src, t0, t1):
-            o = dst[:, t0:t1, :].rearrange("p (c i) j -> p c j i", i=RUN)
-            i = src[:, :, t0:t1].rearrange("p j (c i) -> p c j i", i=RUN)
+        def weave(on_vector, dst, src):
+            o = dst.rearrange("p (c i) j -> p c j i", i=4)
+            i = src.rearrange("p j (c i) -> p c j i", i=4)
             if on_vector:
                 nc.vector.tensor_copy(out=o, in_=i)
             else:
                 nc.scalar.copy(out=o, in_=i)
+
+        def weave_u(on_vector, w, g, t0, t1):
+            weave(on_vector, woven[w, g][:, t0:t1, :], rows[w, g][:, :, t0:t1])
+
+        def scalar_rows(w, g, t0, t1):
+            for j in range(PACK):
+                multiply(False, w, g, j, t0, t1)
+
+        def multiply_woven(w, g, t0, t1):
+            s = SHIFT[w]
+            t0 = max(t0, s)
+            pairs = (t1 - t0) // 2
+            nc.vector.tensor_tensor(
+                out=woven[w, g][:, t0:t1, :].rearrange("p (c i) j -> p c j i", i=2),
+                in0=x_rows(g, t0 - s, t1 - s).rearrange("p j (c i) -> p c j i", i=2),
+                in1=factor[w][:, g, 0:PACK].unsqueeze(1).unsqueeze(3).to_broadcast([P, pairs, PACK, 2]),
+                op=ALU.mult,
+            )
 
         def quantise(codes, scales, src, fmt, t0, t1):
             nc.vector.quantize_mx(
@@ -101,107 +125,163 @@ def tile_mix_three_windows_one_sum_pl_kernel(
                 in_=src[:, t0:t1, :].rearrange("p t j -> p (t j)"),
             )
 
-        def quantise_u(w, g, t0=0, t1=T):
+        def quantise_u(w, g, t0, t1):
             quantise(u_codes[w, g], u_scales[w, g], woven[w, g], U_FORMAT[w], t0, t1)
 
-        def deal_words(w, g):
-            if w == "b":
-                nc.vector.tensor_copy(
-                    out=w_dealt[w, g][:].rearrange("p r (m e) -> p r m e", e=2),
-                    in_=w_raw[w][:, g, :].rearrange("p (m r e) -> p r m e", r=PACK, e=2),
-                )
-            else:
-                nc.vector.tensor_copy(
-                    out=w_dealt[w, g][:].rearrange("p r (c i) -> p c r i", i=RUN),
-                    in_=w_raw[w][:, g, :].rearrange("p (c i r) -> p c r i", r=PACK, i=RUN),
-                )
-
-        def matmuls(w, g, first, last, t0=0, t1=T):
-            for r in range(PACK):
+        def matmuls(w, g, chunks, first=False, last=False):
+            for c in chunks:
                 nc.tensor.matmul_mx(
-                    out=acc[r][:, t0:t1],
-                    lhsT=w_dealt[w, g][:, r, :].bitcast(E2M1 if w == "b" else E4M3),
-                    lhsT_scale=ws_dealt[SCALE_ROW[w] : P, g, r, :],
-                    rhs=u_codes[w, g][:, t0:t1].bitcast(U_FORMAT[w]),
-                    rhs_scale=u_scales[w, g][:, t0:t1],
+                    out=acc[c][:],
+                    lhsT=u_codes[w, g][:, c * P : (c + 1) * P].bitcast(U_FORMAT[w]),
+                    lhsT_scale=u_scales[w, g][:, c * P : (c + 1) * P],
+                    rhs=w_words[w][:, g, :].bitcast(W_FORMAT[w]),
+                    rhs_scale=w_scales[w][:, g, :],
                     start=first,
                     stop=last,
                 )
 
-        x_by_row = xf.rearrange("(g p j) t -> g p j t", g=PASSES, j=PACK)
-        for j in range(PACK):
-            nc.sync.dma_start(out=x_first[j][:], in_=x_by_row[0, :, j, :])
-            if j == 0:
-                for w, src in (("a", fa), ("b", fb), ("c", fd)):
-                    nc.scalar.dma_start(
-                        out=factor[w][:], in_=src.rearrange("(g p j) o -> p g (j o)", g=PASSES, j=PACK)
-                    )
-        nc.gpsimd.memset(ws_raw[:].bitcast(I32), 0)
-        load_scales(nc.gpsimd, "a", wa_scales, range(4))
-        nc.sync.dma_start(out=x_second[0][:], in_=x_by_row[1, :, 0:2, :])
-        load_scales(nc.sync, "b", wb_scales, range(4))
-        nc.sync.dma_start(out=w_raw["b"][:].bitcast(I32), in_=wb_words.rearrange("g p c -> p g c").bitcast(I32))
-        load_scales(nc.sync, "c", wc_scales, range(3))
-        nc.sync.dma_start(out=x_second[1][:], in_=x_by_row[1, :, 2:4, :])
-        load_scales(nc.sync, "c", wc_scales, range(3, 4))
-        nc.sync.dma_start(out=w_raw["c"][:], in_=wc_words.rearrange("g p n e -> p g (n e)").bitcast(I32))
-        nc.sync.dma_start(out=w_raw["a"][:], in_=wa_words.rearrange("g p n e -> p g (n e)").bitcast(I32))
+        def relu(c, r0, r1):
+            nc.scalar.activation(
+                out=z_relu[c][:, r0:r1, :],
+                in_=acc[c][:].rearrange("p (m r) -> p r m", r=PACK)[:, r0:r1, :],
+                func=ACT.Relu,
+            )
 
-        nc.vector.memset(zeros[:], 0.0)
-        for w in "bc":
-            nc.vector.memset(rows[w, 0][:, :, 0:2], 0.0)
-            nc.scalar.activation(out=rows[w, 1][:, :, 0:2], in_=zeros[:], func=ACT.Copy)
+        def turn(c, r0, r1, bank):
+            for r in range(r0, r1):
+                nc.tensor.transpose(turned[bank][:, r, :], z_relu[c][:, r, :], identity[:])
 
-        for j in range(PACK):
-            multiply(False, "a", 0, j)
-            multiply(True, "b", 0, j)
-            multiply(True, "c", 0, j)
-        weave(False, woven["a", 0], rows["a", 0], 0, T)
-        weave(True, woven["b", 0], rows["b", 0], 0, T)
-        weave(True, woven["c", 0], rows["c", 0], 0, T)
-        deal_words("b", 0)
-        quantise_u("b", 0)
-        nc.vector.tensor_copy(out=ws_dealt[:], in_=ws_raw[:].rearrange("p g (m r) -> p g r m", r=PACK))
-        matmuls("b", 0, True, False)
-        quantise_u("c", 0)
-        for w, js in (("b", (0, 1)), ("c", (0, 1)), ("b", (2, 3)), ("c", (2, 3)), ("a", range(PACK))):
-            for j in js:
-                multiply(False, w, 1, j)
-        deal_words("c", 0)
-        matmuls("c", 0, False, False)
-        quantise_u("a", 0)
-        deal_words("a", 0)
-        matmuls("a", 0, False, False)
-        weave(True, woven["b", 1], rows["b", 1], 0, T)
-        deal_words("b", 1)
-        quantise_u("b", 1)
-        matmuls("b", 1, False, False)
-        weave(True, woven["c", 1], rows["c", 1], 0, T)
-        deal_words("c", 1)
-        quantise_u("c", 1)
-        matmuls("c", 1, False, False)
-        deal_words("a", 1)
-        weave(False, woven["a", 1], rows["a", 1], 0, HALF)
-        quantise_u("a", 1, 0, HALF)
-        matmuls("a", 1, False, False, 0, HALF)
-        weave(False, woven["a", 1], rows["a", 1], HALF, T)
-        quantise_u("a", 1, HALF, T)
-        matmuls("a", 1, False, True, HALF, T)
+        def drain(on_vector, c, r0, r1, bank):
+            if on_vector:
+                nc.vector.tensor_copy(out=y[c][:, r0:r1, :], in_=turned[bank][:, r0:r1, :])
+            else:
+                nc.scalar.copy(out=y[c][:, r0:r1, :], in_=turned[bank][:, r0:r1, :])
+
+        def store_y(c):
+            nc.sync.dma_start(out=out_rows[:, :, c * P : (c + 1) * P], in_=y[c][:])
+
+        def weave_y(c):
+            weave(True, y_woven[:, c * P : (c + 1) * P, :], y[c][:])
 
         out_rows = out_0.rearrange("(p r) t -> p r t", r=PACK)
-        for r in range(PACK):
-            if r % 2 == 0:
-                nc.scalar.activation(out=y[:, r, :], in_=acc[r][:], func=ACT.Relu)
-            else:
-                nc.vector.tensor_scalar(out=y[:, r, :], in0=acc[r][:], scalar1=0.0, scalar2=None, op0=ALU.max)
-                nc.sync.dma_start(out=out_rows[:, r - 1 : r + 1, :], in_=y[:, r - 1 : r + 1, :])
-        weave(True, y_woven, y, 0, HALF)
-        weave(False, y_woven, y, HALF, HALF + P)
-        weave(True, y_woven, y, HALF + P, T)
         words_out = out_1[0].rearrange("p t e -> p (t e)").bitcast(I32)
-        for t0 in (0, HALF):
-            quantise(y_codes, y_scales, y_woven, E4M3, t0, t0 + HALF)
-            nc.sync.dma_start(out=words_out[:, t0 : t0 + HALF], in_=y_codes[:, t0 : t0 + HALF])
+        C2, C3 = HALF, HALF + P
+
+        for w in "cba":
+            nc.vector.memset(w_scales[w][:].bitcast(I32), 0)
+        x_by_row = xf.rearrange("(g p j) t -> g p j t", g=PASSES, j=PACK)
+        nc.sync.dma_start(out=x_head[0][:], in_=x_by_row[0, :, 0:2, 0:HALF])
+        for w, src in (("b", fb), ("a", fa), ("c", fd)):
+            nc.scalar.dma_start(
+                out=factor[w][:, :, 0:PACK], in_=src.rearrange("(g p j) o -> p g (j o)", g=PASSES, j=PACK)
+            )
+        nc.sync.dma_start(out=x_head[1][:], in_=x_by_row[0, :, 2:4, 0:HALF])
+        nc.sync.dma_start(out=x_early[:], in_=x_by_row[1, :, :, 0:HALF])
+        load_scales("c", wc_scales, range(2))
+        load_words("c", wc_words.rearrange("g p n e -> p g (n e)"))
+        load_scales("c", wc_scales, range(2, 4))
+        nc.sync.dma_start(out=x_late[0][:, :, LEAD - HALO :], in_=x_by_row[0, :, :, HALF - HALO :])
+        load_words("b", wb_words.rearrange("g p c -> p g c"))
+        load_scales("b", wb_scales, range(4))
+        load_words("a", wa_words.rearrange("g p n e -> p g (n e)"))
+        load_scales("a", wa_scales, range(4))
+        nc.sync.dma_start(out=x_late[1][:, :, LEAD - HALO :], in_=x_by_row[1, :, :, HALF - HALO :])
+
+        make_identity(nc, identity[:])
+        nc.vector.memset(zeros[:], 0.0)
+        nc.vector.memset(rows["c", 0][:, :, 0:HALO], 0.0)
+        nc.vector.memset(woven["c", 1][:, 0:HALO, :], 0.0)
+        for g in range(PASSES):
+            nc.scalar.activation(out=rows["b", g][:, :, 0:HALO], in_=zeros[:], func=ACT.Copy)
+
+        multiply(False, "b", 0, 0, 0, HALF)
+        multiply(False, "b", 0, 1, 0, HALF)
+        multiply(False, "a", 0, 0, 0, HALF)
+        multiply(False, "b", 0, 2, 0, HALF)
+        multiply(False, "b", 0, 3, 0, HALF)
+        multiply(False, "a", 0, 3, 0, HALF)
+        for w, j in (("c", 0), ("c", 1), ("a", 1), ("c", 2), ("c", 3), ("a", 2)):
+            multiply(True, w, 0, j, 0, HALF)
+        weave_u(False, "b", 0, 0, HALF)
+        weave_u(True, "c", 0, 0, HALF)
+        weave_u(True, "a", 0, 0, HALF)
+        quantise_u("c", 0, 0, HALF)
+        matmuls("c", 0, (0, 1), first=True)
+        quantise_u("a", 0, 0, HALF)
+        multiply_woven("c", 1, 0, HALF)
+        quantise_u("b", 0, 0, HALF)
+        quantise_u("c", 1, 0, HALF)
+        matmuls("c", 1, (0, 1))
+        matmuls("b", 0, (0, 1))
+        scalar_rows("b", 1, 0, HALF)
+        multiply(False, "a", 1, 0, 0, HALF)
+        weave_u(False, "b", 1, 0, HALF)
+        for j in range(1, PACK):
+            multiply(False, "a", 1, j, 0, HALF)
+        multiply_woven("a", 0, HALF, T)
+        quantise_u("b", 1, 0, HALF)
+        matmuls("b", 1, (0, 1))
+        weave_u(True, "a", 1, 0, HALF)
+        quantise_u("a", 0, HALF, T)
+        quantise_u("a", 1, 0, HALF)
+        for c in range(2):
+            matmuls("a", 0, (c,))
+            matmuls("a", 1, (c,), last=True)
+        matmuls("a", 0, (2, 3), first=True)
+        scalar_rows("b", 0, HALF, T)
+        weave_u(False, "b", 0, HALF, T)
+        relu(0, 0, PACK)
+        relu(1, 0, PACK)
+        multiply_woven("c", 0, HALF, T)
+        multiply_woven("a", 1, C2, C3)
+        quantise_u("c", 0, HALF, T)
+        matmuls("c", 0, (2, 3))
+        turn(0, 0, PACK, 0)
+        turn(1, 0, PACK, 1)
+        quantise_u("b", 0, HALF, T)
+        matmuls("b", 0, (2, 3))
+        scalar_rows("b", 1, HALF, T)
+        multiply_woven("c", 1, C2, C3)
+        quantise_u("a", 1, C2, C3)
+        matmuls("a", 1, (2,))
+        multiply_woven("a", 1, C3, T)
+        quantise_u("c", 1, C2, C3)
+        matmuls("c", 1, (2,))
+        weave_u(True, "b", 1, C2, C3)
+        quantise_u("a", 1, C3, T)
+        quantise_u("b", 1, C2, C3)
+        matmuls("b", 1, (2,), last=True)
+        matmuls("a", 1, (3,))
+        drain(False, 0, 0, PACK, 0)
+        store_y(0)
+        weave_u(False, "b", 1, C3, T)
+        drain(False, 1, 0, PACK, 1)
+        store_y(1)
+        relu(2, 0, PACK)
+        multiply_woven("c", 1, C3, T)
+        quantise_u("b", 1, C3, T)
+        matmuls("b", 1, (3,))
+        quantise_u("c", 1, C3, T)
+        matmuls("c", 1, (3,), last=True)
+        turn(2, 0, PACK, 2)
+        relu(3, 0, 2)
+        turn(3, 0, 2, 3)
+        relu(3, 2, 4)
+        turn(3, 2, 4, 0)
+        weave_y(0)
+        weave_y(1)
+        quantise(y_codes, y_scales, y_woven, E4M3, 0, HALF)
+        nc.sync.dma_start(out=words_out[:, 0:HALF], in_=y_codes[:, 0:HALF])
+        drain(True, 2, 0, PACK, 2)
+        store_y(2)
+        drain(False, 3, 0, 2, 3)
+        drain(False, 3, 2, 4, 0)
+        store_y(3)
+        weave_y(2)
+        weave_y(3)
+        quantise(y_codes, y_scales, y_woven, E4M3, C2, C3)
+        quantise(y_codes, y_scales, y_woven, E4M3, C3, T)
+        nc.sync.dma_start(out=words_out[:, HALF:T], in_=y_codes[:, HALF:T])
         for q in range(4):
             eng = nc.scalar if q < 2 else nc.sync
             eng.dma_start(

@@ -21,7 +21,6 @@ PACK = 4
 PASSES = K // (P * PACK)
 HALF = T // 2
 HALO = 2
-LEAD = 8
 SHIFT = {"a": 0, "b": 1, "c": 2}
 U_FORMAT = {"a": E4M3, "b": E5M2, "c": E4M3}
 W_FORMAT = {"a": E4M3, "b": E2M1, "c": E4M3}
@@ -44,7 +43,7 @@ def tile_mix_three_windows_one_sum_pl_kernel(
         factor = {w: tile("f_" + w, [P, PASSES, 2 * PACK], F32) for w in "abc"}
         x_head = [tile("x_head%d" % pair, [P, 2, HALF], F32) for pair in range(2)]
         x_early = tile("x_early", [P, PACK, HALF], F32)
-        x_late = [tile("x_late%d" % g, [P, PACK, LEAD + HALF], F32) for g in range(PASSES)]
+        x_late = [tile("x_late%d" % g, [P, PACK, HALF], F32) for g in range(PASSES)]
         rows = {o: tile("rows_%s%d" % o, [P, PACK, T], BF16) for o in ops if o != ("c", 1)}
         woven = {o: tile("woven_%s%d" % o, [P, T, PACK], BF16) for o in ops}
         u_codes = {o: tile("codes_%s%d" % o, [P, T], I32) for o in ops}
@@ -63,7 +62,7 @@ def tile_mix_three_windows_one_sum_pl_kernel(
 
         def x_rows(g, t0, t1):
             if t1 > HALF:
-                return x_late[g][:, :, LEAD + t0 - HALF : LEAD + t1 - HALF]
+                return x_late[g][:, :, t0 - HALF : t1 - HALF]
             return x_early[:, :, t0:t1]
 
         def x_row(g, j, t0, t1):
@@ -81,9 +80,13 @@ def tile_mix_three_windows_one_sum_pl_kernel(
         def load_words(w, src):
             nc.sync.dma_start(out=w_words[w][:].bitcast(I32), in_=src.bitcast(I32))
 
+        def window(w, t0, t1):
+            s = SHIFT[w]
+            return (t0 + s if t0 % HALF == 0 else t0), (t1 + s if t1 == HALF else t1)
+
         def multiply(on_vector, w, g, j, t0, t1):
             s = SHIFT[w]
-            t0 = max(t0, s)
+            t0, t1 = window(w, t0, t1)
             dst = rows[w, g][:, j, t0:t1]
             src = x_row(g, j, t0 - s, t1 - s)
             f = factor[w][:, g, j : j + 1]
@@ -93,8 +96,9 @@ def tile_mix_three_windows_one_sum_pl_kernel(
                 nc.scalar.activation(out=dst, in_=src, func=ACT.Copy, scale=f)
 
         def weave(on_vector, dst, src):
-            o = dst.rearrange("p (c i) j -> p c j i", i=4)
-            i = src.rearrange("p j (c i) -> p c j i", i=4)
+            run = 4 if dst.shape[1] % 4 == 0 else 2
+            o = dst.rearrange("p (c i) j -> p c j i", i=run)
+            i = src.rearrange("p j (c i) -> p c j i", i=run)
             if on_vector:
                 nc.vector.tensor_copy(out=o, in_=i)
             else:
@@ -109,7 +113,7 @@ def tile_mix_three_windows_one_sum_pl_kernel(
 
         def multiply_woven(w, g, t0, t1):
             s = SHIFT[w]
-            t0 = max(t0, s)
+            t0, t1 = window(w, t0, t1)
             pairs = (t1 - t0) // 2
             nc.vector.tensor_tensor(
                 out=woven[w, g][:, t0:t1, :].rearrange("p (c i) j -> p c j i", i=2),
@@ -180,12 +184,12 @@ def tile_mix_three_windows_one_sum_pl_kernel(
         load_scales("c", wc_scales, range(2))
         load_words("c", wc_words.rearrange("g p n e -> p g (n e)"))
         load_scales("c", wc_scales, range(2, 4))
-        nc.sync.dma_start(out=x_late[0][:, :, LEAD - HALO :], in_=x_by_row[0, :, :, HALF - HALO :])
+        nc.sync.dma_start(out=x_late[0][:], in_=x_by_row[0, :, :, HALF:])
         load_words("b", wb_words.rearrange("g p c -> p g c"))
         load_scales("b", wb_scales, range(4))
         load_words("a", wa_words.rearrange("g p n e -> p g (n e)"))
         load_scales("a", wa_scales, range(4))
-        nc.sync.dma_start(out=x_late[1][:, :, LEAD - HALO :], in_=x_by_row[1, :, :, HALF - HALO :])
+        nc.sync.dma_start(out=x_late[1][:], in_=x_by_row[1, :, :, HALF:])
 
         make_identity(nc, identity[:])
         nc.vector.memset(zeros[:], 0.0)
@@ -203,7 +207,7 @@ def tile_mix_three_windows_one_sum_pl_kernel(
         for w, j in (("c", 0), ("c", 1), ("a", 1), ("c", 2), ("c", 3), ("a", 2)):
             multiply(True, w, 0, j, 0, HALF)
         weave_u(False, "b", 0, 0, HALF)
-        weave_u(True, "c", 0, 0, HALF)
+        weave_u(True, "c", 0, 0, HALF + HALO)
         weave_u(True, "a", 0, 0, HALF)
         quantise_u("c", 0, 0, HALF)
         matmuls("c", 0, (0, 1), first=True)
@@ -216,8 +220,9 @@ def tile_mix_three_windows_one_sum_pl_kernel(
         scalar_rows("b", 1, 0, HALF)
         multiply(False, "a", 1, 0, 0, HALF)
         weave_u(False, "b", 1, 0, HALF)
-        for j in range(1, PACK):
-            multiply(False, "a", 1, j, 0, HALF)
+        multiply(False, "a", 1, 1, 0, HALF)
+        for j in (2, 3):
+            multiply(True, "a", 1, j, 0, HALF)
         multiply_woven("a", 0, HALF, T)
         quantise_u("b", 1, 0, HALF)
         matmuls("b", 1, (0, 1))
@@ -233,13 +238,13 @@ def tile_mix_three_windows_one_sum_pl_kernel(
         relu(0, 0, PACK)
         relu(1, 0, PACK)
         multiply_woven("c", 0, HALF, T)
-        multiply_woven("a", 1, C2, C3)
+        quantise_u("b", 0, HALF, T)
         quantise_u("c", 0, HALF, T)
-        matmuls("c", 0, (2, 3))
+        multiply_woven("a", 1, C2, C3)
+        matmuls("b", 0, (2, 3))
         turn(0, 0, PACK, 0)
         turn(1, 0, PACK, 1)
-        quantise_u("b", 0, HALF, T)
-        matmuls("b", 0, (2, 3))
+        matmuls("c", 0, (2, 3))
         scalar_rows("b", 1, HALF, T)
         multiply_woven("c", 1, C2, C3)
         quantise_u("a", 1, C2, C3)

@@ -19,11 +19,16 @@ ALU = mybir.AluOpType
 P = 128
 PACK = 4
 PASSES = K // (P * PACK)
+CHUNKS = T // P
 HALF = T // 2
-HALO = 2
+LAST = T - P
+QUADRANTS = 4
 SHIFT = {"a": 0, "b": 1, "c": 2}
+MAX_SHIFT = 2
 U_FORMAT = {"a": E4M3, "b": E5M2, "c": E4M3}
 W_FORMAT = {"a": E4M3, "b": E2M1, "c": E4M3}
+W_BYTES = {"a": 4, "b": 2, "c": 4}
+ON_VECTOR, ON_SCALAR = True, False
 
 
 def tile_mix_three_windows_one_sum_pl_kernel(
@@ -39,26 +44,31 @@ def tile_mix_three_windows_one_sum_pl_kernel(
         def tile(name, shape, dtype):
             return sb.tile(shape, dtype, name=name, align_bytes=64)
 
-        ops = [(w, g) for w in "abc" for g in range(PASSES)]
+        operands = [(w, g) for w in "abc" for g in range(PASSES)]
         factor = {w: tile("f_" + w, [P, PASSES, 2 * PACK], F32) for w in "abc"}
+        factor_twice = {w: tile("f2_" + w, [P, PASSES, PACK, 2], F32) for w in "ac"}
         x_head = [tile("x_head%d" % pair, [P, 2, HALF], F32) for pair in range(2)]
         x_early = tile("x_early", [P, PACK, HALF], F32)
         x_late = [tile("x_late%d" % g, [P, PACK, HALF], F32) for g in range(PASSES)]
-        rows = {o: tile("rows_%s%d" % o, [P, PACK, T], BF16) for o in ops if o != ("c", 1)}
-        woven = {o: tile("woven_%s%d" % o, [P, T, PACK], BF16) for o in ops}
-        u_codes = {o: tile("codes_%s%d" % o, [P, T], I32) for o in ops}
-        u_scales = {o: tile("scales_%s%d" % o, [P, T], U8) for o in ops}
-        w_words = {w: tile("words_" + w, [P, PASSES, (2 if w == "b" else 4) * N], U8) for w in "abc"}
+        rows = {o: tile("rows_%s%d" % o, [P, PACK, T], BF16) for o in operands if o != ("c", 1)}
+        woven = {o: tile("woven_%s%d" % o, [P, T, PACK], BF16) for o in operands}
+        u_codes = {o: tile("codes_%s%d" % o, [P, T], I32) for o in operands}
+        u_scales = {o: tile("scales_%s%d" % o, [P, T], U8) for o in operands}
+        w_words = {w: tile("words_" + w, [P, PASSES, W_BYTES[w] * N], U8) for w in "abc"}
         w_scales = {w: tile("wscales_" + w, [P, PASSES, N], U8) for w in "abc"}
-        zeros = tile("zeros", [P, PACK, HALO], F32)
+        zeros = tile("zeros", [P, PACK, MAX_SHIFT], F32)
         identity = tile("identity", [P, P], F32)
-        z_relu = [tile("z_relu%d" % c, [P, PACK, P], F32) for c in range(4)]
-        y = [tile("y%d" % c, [P, PACK, P], F32) for c in range(4)]
+        z_relu = [tile("z_relu%d" % c, [P, PACK, P], F32) for c in range(CHUNKS)]
+        y = [tile("y%d" % c, [P, PACK, P], F32) for c in range(CHUNKS)]
         y_woven = tile("y_woven", [P, T, PACK], BF16)
         y_codes = tile("y_codes", [P, T], I32)
         y_scales = tile("y_scales", [P, T], U8)
-        acc = [acc_pool.tile([P, N], F32, name="acc%d" % c) for c in range(4)]
-        turned = [turn_pool.tile([P, PACK, P], F32, name="turned%d" % c) for c in range(4)]
+        acc = [acc_pool.tile([P, N], F32, name="acc%d" % c) for c in range(CHUNKS)]
+        turned = [turn_pool.tile([P, PACK, P], F32, name="turned%d" % c) for c in range(CHUNKS)]
+
+        x_by_row = xf.rearrange("(g p j) t -> g p j t", g=PASSES, j=PACK)
+        out_rows = out_0.rearrange("(p r) t -> p r t", r=PACK)
+        words_out = out_1[0].rearrange("p t e -> p (t e)").bitcast(I32)
 
         def x_rows(g, t0, t1):
             if t1 > HALF:
@@ -70,11 +80,11 @@ def tile_mix_three_windows_one_sum_pl_kernel(
                 return x_head[j // 2][:, j % 2, t0:t1]
             return x_rows(g, t0, t1)[:, j, :]
 
-        def load_scales(w, src, rows_of_quadrant):
-            for r in rows_of_quadrant:
+        def load_scales(w, src, rows_in_quadrant):
+            for r in rows_in_quadrant:
                 nc.sync.dma_start(
                     out=w_scales[w][r:P:32].bitcast(I32),
-                    in_=src.rearrange("g (q r) n -> r q g n", r=4)[r].bitcast(I32),
+                    in_=src.rearrange("g (q r) n -> r q g n", r=PACK)[r].bitcast(I32),
                 )
 
         def load_words(w, src):
@@ -95,31 +105,35 @@ def tile_mix_three_windows_one_sum_pl_kernel(
             else:
                 nc.scalar.activation(out=dst, in_=src, func=ACT.Copy, scale=f)
 
+        def scalar_rows(w, g, t0, t1):
+            for j in range(PACK):
+                multiply(ON_SCALAR, w, g, j, t0, t1)
+
         def weave(on_vector, dst, src):
             run = 4 if dst.shape[1] % 4 == 0 else 2
-            o = dst.rearrange("p (c i) j -> p c j i", i=run)
-            i = src.rearrange("p j (c i) -> p c j i", i=run)
+            dst_walk = dst.rearrange("p (c i) j -> p c j i", i=run)
+            src_walk = src.rearrange("p j (c i) -> p c j i", i=run)
             if on_vector:
-                nc.vector.tensor_copy(out=o, in_=i)
+                nc.vector.tensor_copy(out=dst_walk, in_=src_walk)
             else:
-                nc.scalar.copy(out=o, in_=i)
+                nc.scalar.copy(out=dst_walk, in_=src_walk)
 
         def weave_u(on_vector, w, g, t0, t1):
             weave(on_vector, woven[w, g][:, t0:t1, :], rows[w, g][:, :, t0:t1])
 
-        def scalar_rows(w, g, t0, t1):
-            for j in range(PACK):
-                multiply(False, w, g, j, t0, t1)
-
         def multiply_woven(w, g, t0, t1):
             s = SHIFT[w]
             t0, t1 = window(w, t0, t1)
-            pairs = (t1 - t0) // 2
             nc.vector.tensor_tensor(
                 out=woven[w, g][:, t0:t1, :].rearrange("p (c i) j -> p c j i", i=2),
                 in0=x_rows(g, t0 - s, t1 - s).rearrange("p j (c i) -> p c j i", i=2),
-                in1=factor[w][:, g, 0:PACK].unsqueeze(1).unsqueeze(3).to_broadcast([P, pairs, PACK, 2]),
+                in1=factor_twice[w][:, g, :, :].unsqueeze(1).to_broadcast([P, (t1 - t0) // 2, PACK, 2]),
                 op=ALU.mult,
+            )
+
+        def double_factor(w):
+            nc.vector.tensor_copy(
+                out=factor_twice[w][:], in_=factor[w][:, :, 0:PACK].unsqueeze(3).to_broadcast([P, PASSES, PACK, 2])
             )
 
         def quantise(codes, scales, src, fmt, t0, t1):
@@ -131,6 +145,9 @@ def tile_mix_three_windows_one_sum_pl_kernel(
 
         def quantise_u(w, g, t0, t1):
             quantise(u_codes[w, g], u_scales[w, g], woven[w, g], U_FORMAT[w], t0, t1)
+
+        def quantise_y(t0, t1):
+            quantise(y_codes, y_scales, y_woven, E4M3, t0, t1)
 
         def matmuls(w, g, chunks, first=False, last=False):
             for c in chunks:
@@ -146,8 +163,8 @@ def tile_mix_three_windows_one_sum_pl_kernel(
 
         def relu(c, r0, r1):
             nc.scalar.activation(
-                out=z_relu[c][:, r0:r1, :],
-                in_=acc[c][:].rearrange("p (m r) -> p r m", r=PACK)[:, r0:r1, :],
+                out=z_relu[c][:, r0:r1, :].rearrange("p (h e) m -> p h m e", e=2),
+                in_=acc[c][:].rearrange("p (m h e) -> p h m e", h=2, e=2)[:, r0 // 2 : r1 // 2],
                 func=ACT.Relu,
             )
 
@@ -165,18 +182,16 @@ def tile_mix_three_windows_one_sum_pl_kernel(
             nc.sync.dma_start(out=out_rows[:, :, c * P : (c + 1) * P], in_=y[c][:])
 
         def weave_y(c):
-            weave(True, y_woven[:, c * P : (c + 1) * P, :], y[c][:])
+            weave(ON_VECTOR, y_woven[:, c * P : (c + 1) * P, :], y[c][:])
 
-        out_rows = out_0.rearrange("(p r) t -> p r t", r=PACK)
-        words_out = out_1[0].rearrange("p t e -> p (t e)").bitcast(I32)
-        C2, C3 = HALF, HALF + P
+        def store_words(t0, t1):
+            nc.sync.dma_start(out=words_out[:, t0:t1], in_=y_codes[:, t0:t1])
 
         for w in "cba":
             nc.vector.memset(w_scales[w][:].bitcast(I32), 0)
-        x_by_row = xf.rearrange("(g p j) t -> g p j t", g=PASSES, j=PACK)
         nc.sync.dma_start(out=x_head[0][:], in_=x_by_row[0, :, 0:2, 0:HALF])
-        for w, src in (("b", fb), ("a", fa), ("c", fd)):
-            nc.scalar.dma_start(
+        for w, src, queue in (("b", fb, nc.scalar), ("a", fa, nc.sync), ("c", fd, nc.sync)):
+            queue.dma_start(
                 out=factor[w][:, :, 0:PACK], in_=src.rearrange("(g p j) o -> p g (j o)", g=PASSES, j=PACK)
             )
         nc.sync.dma_start(out=x_head[1][:], in_=x_by_row[0, :, 2:4, 0:HALF])
@@ -193,102 +208,107 @@ def tile_mix_three_windows_one_sum_pl_kernel(
 
         make_identity(nc, identity[:])
         nc.vector.memset(zeros[:], 0.0)
-        nc.vector.memset(rows["c", 0][:, :, 0:HALO], 0.0)
-        nc.vector.memset(woven["c", 1][:, 0:HALO, :], 0.0)
+        nc.vector.memset(rows["c", 0][:, :, 0:MAX_SHIFT], 0.0)
+        nc.vector.memset(woven["c", 1][:, 0:MAX_SHIFT, :], 0.0)
         for g in range(PASSES):
-            nc.scalar.activation(out=rows["b", g][:, :, 0:HALO], in_=zeros[:], func=ACT.Copy)
+            nc.scalar.activation(out=rows["b", g][:, :, 0:MAX_SHIFT], in_=zeros[:], func=ACT.Copy)
 
-        multiply(False, "b", 0, 0, 0, HALF)
-        multiply(False, "b", 0, 1, 0, HALF)
-        multiply(False, "a", 0, 0, 0, HALF)
-        multiply(False, "b", 0, 2, 0, HALF)
-        multiply(False, "b", 0, 3, 0, HALF)
-        multiply(False, "a", 0, 3, 0, HALF)
-        for w, j in (("c", 0), ("c", 1), ("a", 1), ("c", 2), ("c", 3), ("a", 2)):
-            multiply(True, w, 0, j, 0, HALF)
-        weave_u(False, "b", 0, 0, HALF)
-        weave_u(True, "c", 0, 0, HALF + HALO)
-        weave_u(True, "a", 0, 0, HALF)
+
+        for w, j in (("b", 0), ("b", 1), ("a", 0), ("b", 2), ("b", 3), ("a", 3)):
+            multiply(ON_SCALAR, w, 0, j, 0, HALF)
+        double_factor("a")
+        for w, j in (("a", 1), ("c", 0), ("c", 1)):
+            multiply(ON_VECTOR, w, 0, j, 0, HALF)
+        double_factor("c")
+        for w, j in (("c", 2), ("c", 3), ("a", 2)):
+            multiply(ON_VECTOR, w, 0, j, 0, HALF)
+        weave_u(ON_SCALAR, "b", 0, 0, HALF)
+        weave_u(ON_VECTOR, "c", 0, 0, HALF + SHIFT["c"])
+        weave_u(ON_VECTOR, "a", 0, 0, HALF)
         quantise_u("c", 0, 0, HALF)
         matmuls("c", 0, (0, 1), first=True)
         quantise_u("a", 0, 0, HALF)
+
         multiply_woven("c", 1, 0, HALF)
         quantise_u("b", 0, 0, HALF)
         quantise_u("c", 1, 0, HALF)
         matmuls("c", 1, (0, 1))
         matmuls("b", 0, (0, 1))
         scalar_rows("b", 1, 0, HALF)
-        multiply(False, "a", 1, 0, 0, HALF)
-        weave_u(False, "b", 1, 0, HALF)
-        multiply(False, "a", 1, 1, 0, HALF)
+        multiply(ON_SCALAR, "a", 1, 0, 0, HALF)
+        weave_u(ON_SCALAR, "b", 1, 0, HALF)
+        multiply(ON_SCALAR, "a", 1, 1, 0, HALF)
         for j in (2, 3):
-            multiply(True, "a", 1, j, 0, HALF)
+            multiply(ON_VECTOR, "a", 1, j, 0, HALF)
         multiply_woven("a", 0, HALF, T)
         quantise_u("b", 1, 0, HALF)
         matmuls("b", 1, (0, 1))
-        weave_u(True, "a", 1, 0, HALF)
+        weave_u(ON_VECTOR, "a", 1, 0, HALF)
         quantise_u("a", 0, HALF, T)
         quantise_u("a", 1, 0, HALF)
-        for c in range(2):
+        for c in (0, 1):
             matmuls("a", 0, (c,))
             matmuls("a", 1, (c,), last=True)
+
         matmuls("a", 0, (2, 3), first=True)
         scalar_rows("b", 0, HALF, T)
-        weave_u(False, "b", 0, HALF, T)
+        weave_u(ON_SCALAR, "b", 0, HALF, T)
         relu(0, 0, PACK)
         relu(1, 0, PACK)
         multiply_woven("c", 0, HALF, T)
         quantise_u("b", 0, HALF, T)
         quantise_u("c", 0, HALF, T)
-        multiply_woven("a", 1, C2, C3)
+        multiply_woven("a", 1, HALF, LAST)
         matmuls("b", 0, (2, 3))
         turn(0, 0, PACK, 0)
         turn(1, 0, PACK, 1)
         matmuls("c", 0, (2, 3))
+
         scalar_rows("b", 1, HALF, T)
-        multiply_woven("c", 1, C2, C3)
-        quantise_u("a", 1, C2, C3)
+        multiply_woven("c", 1, HALF, LAST)
+        quantise_u("a", 1, HALF, LAST)
         matmuls("a", 1, (2,))
-        multiply_woven("a", 1, C3, T)
-        quantise_u("c", 1, C2, C3)
+        multiply_woven("a", 1, LAST, T)
+        quantise_u("c", 1, HALF, LAST)
         matmuls("c", 1, (2,))
-        weave_u(True, "b", 1, C2, C3)
-        quantise_u("a", 1, C3, T)
-        quantise_u("b", 1, C2, C3)
+        weave_u(ON_VECTOR, "b", 1, HALF, LAST)
+        quantise_u("a", 1, LAST, T)
+        quantise_u("b", 1, HALF, LAST)
         matmuls("b", 1, (2,), last=True)
         matmuls("a", 1, (3,))
-        drain(False, 0, 0, PACK, 0)
+        drain(ON_SCALAR, 0, 0, PACK, 0)
         store_y(0)
-        weave_u(False, "b", 1, C3, T)
-        drain(False, 1, 0, PACK, 1)
+        weave_u(ON_SCALAR, "b", 1, LAST, T)
+        drain(ON_SCALAR, 1, 0, PACK, 1)
         store_y(1)
         relu(2, 0, PACK)
-        multiply_woven("c", 1, C3, T)
-        quantise_u("b", 1, C3, T)
+        multiply_woven("c", 1, LAST, T)
+        quantise_u("b", 1, LAST, T)
         matmuls("b", 1, (3,))
-        quantise_u("c", 1, C3, T)
+        quantise_u("c", 1, LAST, T)
         matmuls("c", 1, (3,), last=True)
+
         turn(2, 0, PACK, 2)
         relu(3, 0, 2)
         turn(3, 0, 2, 3)
-        relu(3, 2, 4)
-        turn(3, 2, 4, 0)
+        relu(3, 2, PACK)
+        turn(3, 2, PACK, 0)
         weave_y(0)
         weave_y(1)
-        quantise(y_codes, y_scales, y_woven, E4M3, 0, HALF)
-        nc.sync.dma_start(out=words_out[:, 0:HALF], in_=y_codes[:, 0:HALF])
-        drain(True, 2, 0, PACK, 2)
+        quantise_y(0, HALF)
+        store_words(0, HALF)
+        drain(ON_VECTOR, 2, 0, PACK, 2)
         store_y(2)
-        drain(False, 3, 0, 2, 3)
-        drain(False, 3, 2, 4, 0)
+        drain(ON_SCALAR, 3, 0, 2, 3)
+        drain(ON_SCALAR, 3, 2, PACK, 0)
         store_y(3)
         weave_y(2)
         weave_y(3)
-        quantise(y_codes, y_scales, y_woven, E4M3, C2, C3)
-        quantise(y_codes, y_scales, y_woven, E4M3, C3, T)
-        nc.sync.dma_start(out=words_out[:, HALF:T], in_=y_codes[:, HALF:T])
-        for q in range(4):
-            eng = nc.scalar if q < 2 else nc.sync
-            eng.dma_start(
+        quantise_y(HALF, LAST)
+        quantise_y(LAST, T)
+        store_words(HALF, T)
+        for q in range(QUADRANTS):
+            queue = nc.scalar if q < QUADRANTS // 2 else nc.sync
+            queue.dma_start(
                 out=out_2[0, 4 * q : 4 * q + 4, :].bitcast(I32), in_=y_scales[32 * q : 32 * q + 4, :].bitcast(I32)
             )

from contextlib import ExitStack

import concourse.mybir as mybir
from concourse.masks import make_identity

K, T, N = 1024, 512, 512
FLOPS = 3 * 2 * K * T * N

F32 = mybir.dt.float32
BF16 = mybir.dt.bfloat16
I32 = mybir.dt.int32
U8 = mybir.dt.uint8
E4M3 = mybir.dt.float8_e4m3fn_x4
E5M2 = mybir.dt.float8_e5m2_x4
E2M1 = mybir.dt.float4_e2m1fn_x4
ACT = mybir.ActivationFunctionType
ALU = mybir.AluOpType

P = 128
PACK = 4
PASSES = K // (P * PACK)
CHUNKS = T // P
HALF = T // 2
LAST = T - P
QUADRANTS = 4
SHIFT = {"a": 0, "b": 1, "c": 2}
MAX_SHIFT = 2
U_FORMAT = {"a": E4M3, "b": E5M2, "c": E4M3}
W_FORMAT = {"a": E4M3, "b": E2M1, "c": E4M3}
W_BYTES = {"a": 4, "b": 2, "c": 4}
ON_VECTOR, ON_SCALAR = True, False


def tile_mix_three_windows_one_sum_pl_kernel(
    tc, xf, fa, fb, fd, wa_words, wa_scales, wb_words, wb_scales, wc_words, wc_scales, out_0, out_1, out_2
):
    nc = tc.nc
    with ExitStack() as ctx:
        sb = ctx.enter_context(tc.tile_pool(name="sb", bufs=1))
        acc_pool = ctx.enter_context(tc.psum_pool(name="acc", bufs=1))
        turn_pool = ctx.enter_context(tc.psum_pool(name="turn", bufs=1))
        ctx.enter_context(tc.manual_schedule())

        def tile(name, shape, dtype):
            return sb.tile(shape, dtype, name=name, align_bytes=64)

        operands = [(w, g) for w in "abc" for g in range(PASSES)]
        factor = {w: tile("f_" + w, [P, PASSES, 2 * PACK], F32) for w in "abc"}
        factor_twice = {w: tile("f2_" + w, [P, PASSES, PACK, 2], F32) for w in "ac"}
        x_head = [tile("x_head%d" % pair, [P, 2, HALF], F32) for pair in range(2)]
        x_early = tile("x_early", [P, PACK, HALF], F32)
        x_late = [tile("x_late%d" % g, [P, PACK, HALF], F32) for g in range(PASSES)]
        rows = {o: tile("rows_%s%d" % o, [P, PACK, T], BF16) for o in operands if o != ("c", 1)}
        woven = {o: tile("woven_%s%d" % o, [P, T, PACK], BF16) for o in operands}
        u_codes = {o: tile("codes_%s%d" % o, [P, T], I32) for o in operands}
        u_scales = {o: tile("scales_%s%d" % o, [P, T], U8) for o in operands}
        w_words = {w: tile("words_" + w, [P, PASSES, W_BYTES[w] * N], U8) for w in "abc"}
        w_scales = {w: tile("wscales_" + w, [P, PASSES, N], U8) for w in "abc"}
        zeros = tile("zeros", [P, PACK, MAX_SHIFT], F32)
        identity = tile("identity", [P, P], F32)
        z_relu = [tile("z_relu%d" % c, [P, PACK, P], F32) for c in range(CHUNKS)]
        y = [tile("y%d" % c, [P, PACK, P], F32) for c in range(CHUNKS)]
        y_woven = tile("y_woven", [P, T, PACK], BF16)
        y_codes = tile("y_codes", [P, T], I32)
        y_scales = tile("y_scales", [P, T], U8)
        acc = [acc_pool.tile([P, N], F32, name="acc%d" % c) for c in range(CHUNKS)]
        turned = [turn_pool.tile([P, PACK, P], F32, name="turned%d" % c) for c in range(CHUNKS)]

        x_by_row = xf.rearrange("(g p j) t -> g p j t", g=PASSES, j=PACK)
        out_rows = out_0.rearrange("(p r) t -> p r t", r=PACK)
        words_out = out_1[0].rearrange("p t e -> p (t e)").bitcast(I32)

        def x_rows(g, t0, t1):
            if t1 > HALF:
                return x_late[g][:, :, t0 - HALF : t1 - HALF]
            return x_early[:, :, t0:t1]

        def x_row(g, j, t0, t1):
            if g == 0 and t1 <= HALF:
                return x_head[j // 2][:, j % 2, t0:t1]
            return x_rows(g, t0, t1)[:, j, :]

        def load_scales(w, src, rows_in_quadrant):
            for r in rows_in_quadrant:
                nc.sync.dma_start(
                    out=w_scales[w][r:P:32].bitcast(I32),
                    in_=src.rearrange("g (q r) n -> r q g n", r=PACK)[r].bitcast(I32),
                )

        def load_words(w, src):
            nc.sync.dma_start(out=w_words[w][:].bitcast(I32), in_=src.bitcast(I32))

        def window(w, t0, t1):
            s = SHIFT[w]
            return (t0 + s if t0 % HALF == 0 else t0), (t1 + s if t1 == HALF else t1)

        def multiply(on_vector, w, g, j, t0, t1):
            s = SHIFT[w]
            t0, t1 = window(w, t0, t1)
            dst = rows[w, g][:, j, t0:t1]
            src = x_row(g, j, t0 - s, t1 - s)
            f = factor[w][:, g, j : j + 1]
            if on_vector:
                nc.vector.tensor_scalar(out=dst, in0=src, scalar1=f, scalar2=None, op0=ALU.mult)
            else:
                nc.scalar.activation(out=dst, in_=src, func=ACT.Copy, scale=f)

        def scalar_rows(w, g, t0, t1):
            for j in range(PACK):
                multiply(ON_SCALAR, w, g, j, t0, t1)

        def weave(on_vector, dst, src):
            run = 4 if dst.shape[1] % 4 == 0 else 2
            dst_walk = dst.rearrange("p (c i) j -> p c j i", i=run)
            src_walk = src.rearrange("p j (c i) -> p c j i", i=run)
            if on_vector:
                nc.vector.tensor_copy(out=dst_walk, in_=src_walk)
            else:
                nc.scalar.copy(out=dst_walk, in_=src_walk)

        def weave_u(on_vector, w, g, t0, t1):
            weave(on_vector, woven[w, g][:, t0:t1, :], rows[w, g][:, :, t0:t1])

        def multiply_woven(w, g, t0, t1):
            s = SHIFT[w]
            t0, t1 = window(w, t0, t1)
            nc.vector.tensor_tensor(
                out=woven[w, g][:, t0:t1, :].rearrange("p (c i) j -> p c j i", i=2),
                in0=x_rows(g, t0 - s, t1 - s).rearrange("p j (c i) -> p c j i", i=2),
                in1=factor_twice[w][:, g, :, :].unsqueeze(1).to_broadcast([P, (t1 - t0) // 2, PACK, 2]),
                op=ALU.mult,
            )

        def double_factor(w):
            nc.vector.tensor_copy(
                out=factor_twice[w][:], in_=factor[w][:, :, 0:PACK].unsqueeze(3).to_broadcast([P, PASSES, PACK, 2])
            )

        def quantise(codes, scales, src, fmt, t0, t1):
            nc.vector.quantize_mx(
                out=codes[:, t0:t1].bitcast(fmt),
                scales=scales[:, t0:t1],
                in_=src[:, t0:t1, :].rearrange("p t j -> p (t j)"),
            )

        def quantise_u(w, g, t0, t1):
            quantise(u_codes[w, g], u_scales[w, g], woven[w, g], U_FORMAT[w], t0, t1)

        def quantise_y(t0, t1):
            quantise(y_codes, y_scales, y_woven, E4M3, t0, t1)

        def matmuls(w, g, chunks, first=False, last=False):
            for c in chunks:
                nc.tensor.matmul_mx(
                    out=acc[c][:],
                    lhsT=u_codes[w, g][:, c * P : (c + 1) * P].bitcast(U_FORMAT[w]),
                    lhsT_scale=u_scales[w, g][:, c * P : (c + 1) * P],
                    rhs=w_words[w][:, g, :].bitcast(W_FORMAT[w]),
                    rhs_scale=w_scales[w][:, g, :],
                    start=first,
                    stop=last,
                )

        def relu(c, r0, r1):
            nc.scalar.activation(
                out=z_relu[c][:, r0:r1, :].rearrange("p (h e) m -> p h m e", e=2),
                in_=acc[c][:].rearrange("p (m h e) -> p h m e", h=2, e=2)[:, r0 // 2 : r1 // 2],
                func=ACT.Relu,
            )

        def turn(c, r0, r1, bank):
            for r in range(r0, r1):
                nc.tensor.transpose(turned[bank][:, r, :], z_relu[c][:, r, :], identity[:])

        def drain(on_vector, c, r0, r1, bank):
            if on_vector:
                nc.vector.tensor_copy(out=y[c][:, r0:r1, :], in_=turned[bank][:, r0:r1, :])
            else:
                nc.scalar.copy(out=y[c][:, r0:r1, :], in_=turned[bank][:, r0:r1, :])

        def store_y(c):
            nc.sync.dma_start(out=out_rows[:, :, c * P : (c + 1) * P], in_=y[c][:])

        def weave_y(c):
            weave(ON_VECTOR, y_woven[:, c * P : (c + 1) * P, :], y[c][:])

        def store_words(t0, t1):
            nc.sync.dma_start(out=words_out[:, t0:t1], in_=y_codes[:, t0:t1])

        for w in "cba":
            nc.vector.memset(w_scales[w][:].bitcast(I32), 0)
        nc.sync.dma_start(out=x_head[0][:], in_=x_by_row[0, :, 0:2, 0:HALF])
        for w, src, queue in (("b", fb, nc.scalar), ("a", fa, nc.sync), ("c", fd, nc.sync)):
            queue.dma_start(
                out=factor[w][:, :, 0:PACK], in_=src.rearrange("(g p j) o -> p g (j o)", g=PASSES, j=PACK)
            )
        nc.sync.dma_start(out=x_head[1][:], in_=x_by_row[0, :, 2:4, 0:HALF])
        nc.sync.dma_start(out=x_early[:], in_=x_by_row[1, :, :, 0:HALF])
        load_scales("c", wc_scales, range(2))
        load_words("c", wc_words.rearrange("g p n e -> p g (n e)"))
        load_scales("c", wc_scales, range(2, 4))
        nc.sync.dma_start(out=x_late[0][:], in_=x_by_row[0, :, :, HALF:])
        load_words("b", wb_words.rearrange("g p c -> p g c"))
        load_scales("b", wb_scales, range(4))
        load_words("a", wa_words.rearrange("g p n e -> p g (n e)"))
        load_scales("a", wa_scales, range(4))
        nc.sync.dma_start(out=x_late[1][:], in_=x_by_row[1, :, :, HALF:])

        make_identity(nc, identity[:])
        nc.vector.memset(zeros[:], 0.0)
        nc.vector.memset(rows["c", 0][:, :, 0:MAX_SHIFT], 0.0)
        nc.vector.memset(woven["c", 1][:, 0:MAX_SHIFT, :], 0.0)
        for g in range(PASSES):
            nc.scalar.activation(out=rows["b", g][:, :, 0:MAX_SHIFT], in_=zeros[:], func=ACT.Copy)


        for w, j in (("b", 0), ("b", 1), ("a", 0), ("b", 2), ("b", 3), ("a", 3)):
            multiply(ON_SCALAR, w, 0, j, 0, HALF)
        double_factor("a")
        for w, j in (("a", 1), ("c", 0), ("c", 1)):
            multiply(ON_VECTOR, w, 0, j, 0, HALF)
        double_factor("c")
        for w, j in (("c", 2), ("c", 3), ("a", 2)):
            multiply(ON_VECTOR, w, 0, j, 0, HALF)
        weave_u(ON_SCALAR, "b", 0, 0, HALF)
        weave_u(ON_VECTOR, "c", 0, 0, HALF + SHIFT["c"])
        weave_u(ON_VECTOR, "a", 0, 0, HALF)
        quantise_u("c", 0, 0, HALF)
        matmuls("c", 0, (0, 1), first=True)
        quantise_u("a", 0, 0, HALF)

        multiply_woven("c", 1, 0, HALF)
        quantise_u("b", 0, 0, HALF)
        quantise_u("c", 1, 0, HALF)
        matmuls("c", 1, (0, 1))
        matmuls("b", 0, (0, 1))
        scalar_rows("b", 1, 0, HALF)
        multiply(ON_SCALAR, "a", 1, 0, 0, HALF)
        weave_u(ON_SCALAR, "b", 1, 0, HALF)
        multiply(ON_SCALAR, "a", 1, 1, 0, HALF)
        for j in (2, 3):
            multiply(ON_VECTOR, "a", 1, j, 0, HALF)
        multiply_woven("a", 0, HALF, T)
        quantise_u("b", 1, 0, HALF)
        matmuls("b", 1, (0, 1))
        weave_u(ON_VECTOR, "a", 1, 0, HALF)
        quantise_u("a", 0, HALF, T)
        quantise_u("a", 1, 0, HALF)
        for c in (0, 1):
            matmuls("a", 0, (c,))
            matmuls("a", 1, (c,), last=True)

        matmuls("a", 0, (2, 3), first=True)
        scalar_rows("b", 0, HALF, T)
        weave_u(ON_SCALAR, "b", 0, HALF, T)
        relu(0, 0, PACK)
        relu(1, 0, PACK)
        multiply_woven("c", 0, HALF, T)
        quantise_u("b", 0, HALF, T)
        quantise_u("c", 0, HALF, T)
        multiply_woven("a", 1, HALF, LAST)
        matmuls("b", 0, (2, 3))
        turn(0, 0, PACK, 0)
        turn(1, 0, PACK, 1)
        matmuls("c", 0, (2, 3))

        scalar_rows("b", 1, HALF, T)
        multiply_woven("c", 1, HALF, LAST)
        quantise_u("a", 1, HALF, LAST)
        matmuls("a", 1, (2,))
        multiply_woven("a", 1, LAST, T)
        quantise_u("c", 1, HALF, LAST)
        matmuls("c", 1, (2,))
        weave_u(ON_VECTOR, "b", 1, HALF, LAST)
        quantise_u("a", 1, LAST, T)
        quantise_u("b", 1, HALF, LAST)
        matmuls("b", 1, (2,), last=True)
        matmuls("a", 1, (3,))
        drain(ON_SCALAR, 0, 0, PACK, 0)
        store_y(0)
        weave_u(ON_SCALAR, "b", 1, LAST, T)
        drain(ON_SCALAR, 1, 0, PACK, 1)
        store_y(1)
        relu(2, 0, PACK)
        multiply_woven("c", 1, LAST, T)
        quantise_u("b", 1, LAST, T)
        matmuls("b", 1, (3,))
        quantise_u("c", 1, LAST, T)
        matmuls("c", 1, (3,), last=True)

        turn(2, 0, PACK, 2)
        relu(3, 0, 2)
        turn(3, 0, 2, 3)
        relu(3, 2, PACK)
        turn(3, 2, PACK, 0)
        weave_y(0)
        weave_y(1)
        quantise_y(0, HALF)
        store_words(0, HALF)
        drain(ON_VECTOR, 2, 0, PACK, 2)
        store_y(2)
        drain(ON_SCALAR, 3, 0, 2, 3)
        drain(ON_SCALAR, 3, 2, PACK, 0)
        store_y(3)
        weave_y(2)
        weave_y(3)
        quantise_y(HALF, LAST)
        quantise_y(LAST, T)
        store_words(HALF, T)
        for q in range(QUADRANTS):
            queue = nc.scalar if q < QUADRANTS // 2 else nc.sync
            queue.dma_start(
                out=out_2[0, 4 * q : 4 * q + 4, :].bitcast(I32), in_=y_scales[32 * q : 32 * q + 4, :].bitcast(I32)
            )
